import numpy as np
import ml_dtypes


def mxq(x, axis, fmt="e4m3"):
    dtype, down = {"e4m3": (ml_dtypes.float8_e4m3fn, 7), "e5m2": (ml_dtypes.float8_e5m2, 14)}[fmt]
    v = np.moveaxis(np.asarray(x, np.float32).astype(ml_dtypes.bfloat16).astype(np.float64), axis, -1)
    blocks = v.reshape(v.shape[:-1] + (-1, 32))
    amax = np.abs(blocks).max(-1, keepdims=True)
    byte = np.maximum(np.where(amax > 0, np.frexp(amax)[1] - 1 + 127, 0) - down, 1)
    scale = np.exp2(byte - 127.0)
    codes = (blocks / scale).astype(np.float32).astype(dtype).astype(np.float64)
    return np.moveaxis((codes * scale).reshape(v.shape), -1, axis)


WIDE = False


def mx_kscale(k):
    if not WIDE:
        return np.ones(k)
    levels = np.array([10, -10, 5, -5, 0])
    if k % 512:
        return np.exp2(np.random.permutation(np.resize(levels, k // 32))).repeat(32)
    a = np.empty((k // 512, 16))
    for p in range(k // 512):
        a[p, :8] = np.random.permutation(np.resize(levels, 8))
        for g in range(8):
            far = levels[np.abs(levels - a[p, g]) >= 10]
            a[p, g + 8] = far[np.random.randint(len(far))]
    return np.exp2(a.ravel()).repeat(32)


def f64(x):
    return np.asarray(x).astype(np.float64)


def striped8(idx):
    return np.concatenate([x.reshape(-1, 16).T for x in idx]).astype(np.uint16)


def runs(offs, k):
    lists = np.stack([offs[16 * r : 16 * r + 16].T.reshape(-1) for r in range(8)]).astype(np.int64)
    return lists[np.arange(k) % 512 // 64]


def pack_weight(w):
    k, n = w.shape
    w = f64(np.asarray(w, np.float32).astype(ml_dtypes.bfloat16)).reshape(k // 32, 32, n)
    amax = np.abs(w).max(1)
    byte = np.clip(np.where(amax > 0, np.frexp(amax)[1] - 1 + 127 - 7, 1), 1, 254)
    scaled = (w * np.exp2(127.0 - byte)[:, None, :]).reshape(k, n).astype(np.float32)
    words = np.ascontiguousarray(scaled.reshape(k // 512, 128, 4, n).transpose(0, 1, 3, 2)).astype(ml_dtypes.float8_e4m3fn).view(np.uint8)
    return words, np.ascontiguousarray(byte.astype(np.uint8).reshape(k // 512, 16, n))


def unpack_weight(words, scales):
    g, p, n, _ = words.shape
    vals = np.ascontiguousarray(words).view(ml_dtypes.float8_e4m3fn).astype(np.float64) * np.repeat(np.exp2(scales.astype(np.float64) - 127.0), 8, axis=1)[..., None]
    return vals.transpose(0, 1, 3, 2).reshape(g * 512, n)


def relu(v):
    return np.maximum(v, 0.0)


K, T, S, N, H = 512, 2048, 512, 512, 512


def setup_inputs():
    n = np.random.standard_normal
    s = mx_kscale(K)[:, None]
    u = mx_kscale(H)
    packed_xT = pack_weight(n((K, T)) * s)
    return {
        "x_words": packed_xT[0],
        "x_scales": packed_xT[1],
        "w1": (n((K, H)) / np.sqrt(K) / s * u).astype(np.float32),
        "w2": (n((K, H)) / np.sqrt(K) / s).astype(np.float32),
        "w3": (n((H, N)) / np.sqrt(2 * H) / u[:, None]).astype(np.float32),
        "w4": (n((H, N)) / np.sqrt(2 * H) / u[:, None]).astype(np.float32),
        "offs": striped8(np.stack([np.random.permutation(T)[:S] for _ in range(8)])),
        "p1": striped8(np.stack([np.random.permutation(S) for _ in range(8)])),
        "p2": striped8(np.stack([np.random.permutation(S) for _ in range(8)])),
    }


def reference(x_words, x_scales, w1, w2, w3, w4, offs, p1, p2):
    xq = unpack_weight(x_words, x_scales)[np.arange(K)[:, None], runs(offs, K)]
    y = mxq(f64(w1), 0, "e4m3").T @ xq
    e = mxq(f64(w2), 0, "e4m3").T @ xq
    z = y * (0.5 * (e[np.arange(H)[:, None], runs(p1, H)] + e[np.arange(H)[:, None], runs(p2, H)]))
    o = mxq(f64(w3), 0, "e4m3").T @ mxq(y, 0, "e4m3") + mxq(f64(w4), 0, "e4m3").T @ mxq(z, 0, "e4m3")
    return relu(o)

@@ -1,0 +1,240 @@
+from contextlib import ExitStack
+
+import concourse.mybir as mybir
+
+K, T, S, N, H = 512, 2048, 512, 512, 512
+FLOPS = 2 * K * H * S * 2 + 2 * H * N * S * 2
+
+F32 = mybir.dt.float32
+BF16 = mybir.dt.bfloat16
+I32 = mybir.dt.int32
+U32 = mybir.dt.uint32
+U16 = mybir.dt.uint16
+U8 = mybir.dt.uint8
+FP8X4 = mybir.dt.float8_e4m3fn_x4
+ACT = mybir.ActivationFunctionType
+ALU = mybir.AluOpType
+
+P = 128
+PACK = 4
+BLK = 128
+HALF = S // 2
+CHUNKS = ((0, 256), (256, 128), (384, 128))
+
+
+def tile_picked_pnn8_relu_p_kernel(
+    tc, x_words, x_scales, w1, w2, w3, w4, offs, p1, p2, out
+):
+    nc = tc.nc
+    with ExitStack() as ctx:
+        lists = ctx.enter_context(tc.tile_pool(name="lists", bufs=1))
+        keep = ctx.enter_context(tc.tile_pool(name="keep", bufs=1))
+        psum = ctx.enter_context(tc.psum_pool(name="psum", bufs=1))
+
+        offs_t = lists.tile([P, S // 16], U16, name="offs_t")
+        p1_t = lists.tile([P, S // 16], U16, name="p1_t")
+        p2_t = lists.tile([P, S // 16], U16, name="p2_t")
+
+        def sb(name, shape, dtype, tag=None):
+            return keep.tile(shape, dtype, name=name, tag=tag or name, align_bytes=64)
+
+        def load_weight(name, w, tag=None):
+            raw = sb(name + "_raw", [P, PACK, 512], F32, tag)
+            nc.sync.dma_start(out=raw[:], in_=w.rearrange("(p j) c -> p j c", j=PACK))
+            return raw
+
+        def cast_dealt(copy, name, raw, tag):
+            grouped = sb(name + "_bf", [P, PACK * 512], BF16, tag)
+            copy(
+                out=grouped[:].rearrange("p (t m j) -> p m j t", t=PACK, j=PACK),
+                in_=raw[:].rearrange("p j (m t) -> p m j t", t=PACK),
+            )
+            return grouped
+
+        def cast_plain(copy, name, raw):
+            grouped = sb(name + "_bf", [P, PACK * 512], BF16)
+            copy(
+                out=grouped[:].rearrange("p (c i j) -> p c j i", i=4, j=PACK),
+                in_=raw[:].rearrange("p j (c i) -> p c j i", i=4),
+            )
+            return grouped
+
+        def quantize(name, grouped, width):
+            codes = sb(name + "_codes", [P, width], U32)
+            scales = sb(name + "_scales", [P, width], U8)
+            nc.vector.quantize_mx(out=codes[:].bitcast(FP8X4), scales=scales[:], in_=grouped)
+            return codes, scales
+
+        def mx(acc, lhs, lcols, rcodes, rscales, start, stop):
+            nc.tensor.matmul_mx(
+                out=acc,
+                lhsT=lhs[0][:, lcols].bitcast(FP8X4),
+                lhsT_scale=lhs[1][:, lcols],
+                rhs=rcodes.bitcast(FP8X4),
+                rhs_scale=rscales,
+                start=start,
+                stop=stop,
+            )
+
+        scale_table = sb("scale_table", [P, T], U8)
+        nc.vector.memset(scale_table[:].bitcast(I32), 0)
+        warm = sb("warm", [P, 8], F32)
+        nc.vector.memset(warm[:], 0.0)
+        nc.sync.dma_start(out=offs_t[:], in_=offs)
+        for r in range(2):
+            nc.scalar.dma_start(
+                out=scale_table[:].bitcast(I32)[r:P:16, :], in_=x_scales[0].bitcast(I32)[r:16:2, :]
+            )
+        warm2 = sb("warm2", [P, 8], F32)
+        nc.scalar.activation(out=warm2[:], in_=warm[:], func=ACT.Relu)
+        w2_raw = load_weight("w2", w2)
+        nc.sync.dma_start(out=p1_t[:], in_=p1)
+        nc.sync.dma_start(out=p2_t[:], in_=p2)
+        word_table = sb("word_table", [P, T], U32)
+        nc.sync.dma_start(
+            out=word_table[:].bitcast(I32), in_=x_words[0].rearrange("p n t -> p (n t)").bitcast(I32)
+        )
+
+        picked_scales = sb("picked_scales", [P, S], U8)
+        nc.vector.tensor_copy(out=picked_scales[:], in_=scale_table[:].indirect(offs_t[:]))
+        x_plane = sb("x_plane", [P, S], U8)
+        nc.vector.tensor_copy(out=x_plane[:].bitcast(I32), in_=picked_scales[:].bitcast(I32))
+        for r in range(2):
+            nc.scalar.dma_start(
+                out=x_plane[:].bitcast(I32)[2 + r : P : 32, :],
+                in_=picked_scales[:].bitcast(I32)[16 + r : P : 32, :],
+            )
+
+        w2q = quantize("w2", cast_dealt(nc.vector.tensor_copy, "w2", w2_raw, "scale_table")[:], 512)
+
+        w1_raw = load_weight("w1", w1, "w2_raw")
+        w3_raw = load_weight("w3", w3, "scale_table")
+        x_codes = []
+        for h in range(2):
+            codes = sb("x_codes%d" % h, [P, HALF], U32)
+            nc.vector.tensor_copy(
+                out=codes[:], in_=word_table[:].indirect(offs_t[:, h * HALF // 16 : (h + 1) * HALF // 16])
+            )
+            x_codes.append(codes)
+
+        w4_raw = load_weight("w4", w4, "word_table")
+        e_banks = [psum.tile([P, S], F32, name="e_bank%d" % t, tag="a%d" % t) for t in range(PACK)]
+        for t, h in ((0, 0), (1, 0), (0, 1), (1, 1), (2, 0), (2, 1), (3, 0), (3, 1)):
+            cols = slice(h * HALF, (h + 1) * HALF)
+            mx(e_banks[t][:, cols], w2q, slice(t * P, (t + 1) * P), x_codes[h][:], x_plane[:, cols], True, True)
+        e_rows = []
+        for t in range(PACK):
+            row = sb("e_row%d" % t, [P, S], F32)
+            nc.scalar.activation(out=row[:], in_=e_banks[t][:], func=ACT.Copy, scale=0.5)
+            e_rows.append(row)
+
+        w1_bf = cast_dealt(nc.scalar.copy, "w1", w1_raw, "w2_codes")
+
+        def gather_first(c, first, t):
+            j0, n = CHUNKS[c]
+            nc.vector.tensor_copy(
+                out=first[:, t, :], in_=e_rows[t][:].indirect(p1_t[:, j0 // 16 : (j0 + n) // 16])
+            )
+
+        def gather_add(c, first, both, t):
+            j0, n = CHUNKS[c]
+            nc.vector.tensor_tensor(
+                out=both[:, t, :],
+                in0=e_rows[t][:].indirect(p2_t[:, j0 // 16 : (j0 + n) // 16]),
+                in1=first[:, t, :],
+                op=ALU.add,
+            )
+
+        first0 = sb("first0", [P, PACK, 256], F32)
+        both0 = sb("both0", [P, PACK, 256], F32, "both")
+        gather_first(0, first0, 0)
+        for t in range(1, PACK):
+            gather_first(0, first0, t)
+            gather_add(0, first0, both0, t - 1)
+        gather_add(0, first0, both0, PACK - 1)
+
+        w1q = quantize("w1", w1_bf[:], 512)
+        w3_bf = cast_plain(nc.scalar.copy, "w3", w3_raw)
+
+        y_banks = []
+        for b in range(S // BLK):
+            bank = psum.tile([P, PACK, BLK], F32, name="y_bank%d" % b, tag="b%d" % b)
+            h, lo = divmod(b * BLK, HALF)
+            for t in range(PACK):
+                mx(
+                    bank[:, t, :], w1q, slice(t * P, (t + 1) * P),
+                    x_codes[h][:, lo : lo + BLK], x_plane[:, b * BLK : (b + 1) * BLK], True, True,
+                )
+            y_banks.append(bank)
+
+        y_bf = []
+        for c, (j0, n) in enumerate(CHUNKS):
+            tile = sb("y_bf%d" % c, [P, n * PACK], BF16)
+            for b in range(n // BLK):
+                nc.scalar.copy(
+                    out=tile[:, b * BLK * PACK : (b + 1) * BLK * PACK].rearrange("p (j t) -> p j t", t=PACK),
+                    in_=y_banks[j0 // BLK + b][:].rearrange("p t j -> p j t"),
+                )
+            y_bf.append(tile)
+
+        w4_bf = cast_plain(nc.scalar.copy, "w4", w4_raw)
+
+        def product(c, both):
+            j0, n = CHUNKS[c]
+            tile = sb("z_bf%d" % c, [P, n * PACK], BF16)
+            for b in range(n // BLK):
+                nc.vector.tensor_tensor(
+                    out=tile[:, b * BLK * PACK : (b + 1) * BLK * PACK].rearrange(
+                        "p (c i t) -> p c t i", i=4, t=PACK
+                    ),
+                    in0=y_banks[j0 // BLK + b][:].rearrange("p t (c i) -> p c t i", i=4),
+                    in1=both[:, :, b * BLK : (b + 1) * BLK].rearrange("p t (c i) -> p c t i", i=4),
+                    op=ALU.mult,
+                )
+            return tile
+
+        def finish(c, w3q, w4q, yq, zq):
+            j0, n = CHUNKS[c]
+            accs = [psum.tile([P, n], F32, name="o%d_%d" % (c, m), tag="a%d" % m) for m in range(N // P)]
+            for m in range(N // P):
+                mx(accs[m][:], w3q, slice(m * P, (m + 1) * P), yq[0][:], yq[1][:], True, False)
+            for m in range(N // P):
+                mx(accs[m][:], w4q, slice(m * P, (m + 1) * P), zq[0][:], zq[1][:], False, True)
+            last = c == len(CHUNKS) - 1
+            for pair in range(2):
+                res = sb("res%d_%d" % (c, pair), [P, 2, n], F32)
+                for i in range(2):
+                    m = 2 * pair + i
+                    if last and pair == 1:
+                        nc.vector.tensor_scalar_max(out=res[:, i, :], in0=accs[m][:], scalar1=0.0)
+                    else:
+                        nc.scalar.activation(out=res[:, i, :], in_=accs[m][:], func=ACT.Relu)
+                nc.sync.dma_start(
+                    out=out[2 * pair * P : (2 * pair + 2) * P, j0 : j0 + n].rearrange("(i p) j -> p i j", p=P),
+                    in_=res[:],
+                )
+
+        first1 = sb("first1", [P, PACK, 128], F32, "w2_codes")
+        for t in range(PACK):
+            gather_first(1, first1, t)
+        z0 = product(0, both0)
+        both1 = sb("both1", [P, PACK, 128], F32, "both")
+        for t in range(PACK):
+            gather_add(1, first1, both1, t)
+        w3q = quantize("w3", w3_bf[:], 512)
+        yq = [quantize("y%d" % c, y_bf[c][:], CHUNKS[c][1]) for c in range(len(CHUNKS))]
+        zq0 = quantize("z0", z0[:], 256)
+        z1 = product(1, both1)
+        first2 = sb("first2", [P, PACK, 128], F32, "w3_bf")
+        for t in range(PACK):
+            gather_first(2, first2, t)
+        w4q = quantize("w4", w4_bf[:], 512)
+        zq1 = quantize("z1", z1[:], 128)
+        finish(0, w3q, w4q, yq[0], zq0)
+        finish(1, w3q, w4q, yq[1], zq1)
+        both2 = sb("both2", [P, PACK, 128], F32, "w4_bf")
+        for t in range(PACK):
+            gather_add(2, first2, both2, t)
+        z2 = product(2, both2)
+        zq2 = quantize("z2", z2[:], 128)
+        finish(2, w3q, w4q, yq[2], zq2)

@@ -77,35 +77,41 @@ def tile_picked_pnn8_relu_p_kernel(
             )
 
         scale_table = sb("scale_table", [P, T], U8)
-        nc.vector.memset(scale_table[:].bitcast(I32), 0)
         warm = sb("warm", [P, 8], F32)
         nc.vector.memset(warm[:], 0.0)
         nc.sync.dma_start(out=offs_t[:], in_=offs)
-        for r in range(2):
-            nc.scalar.dma_start(
-                out=scale_table[:].bitcast(I32)[r:P:16, :], in_=x_scales[0].bitcast(I32)[r:16:2, :]
-            )
+        nc.sync.dma_start(
+            out=scale_table[:].bitcast(I32),
+            in_=x_scales[0].bitcast(I32).unsqueeze(1).to_broadcast([16, 8, T // 4]),
+        )
         warm2 = sb("warm2", [P, 8], F32)
         nc.scalar.activation(out=warm2[:], in_=warm[:], func=ACT.Relu)
         w2_raw = load_weight("w2", w2)
-        nc.sync.dma_start(out=p1_t[:], in_=p1)
-        nc.sync.dma_start(out=p2_t[:], in_=p2)
         word_table = sb("word_table", [P, T], U32)
         nc.sync.dma_start(
             out=word_table[:].bitcast(I32), in_=x_words[0].rearrange("p n t -> p (n t)").bitcast(I32)
         )
+        nc.sync.dma_start(out=p1_t[:], in_=p1)
+        nc.sync.dma_start(out=p2_t[:], in_=p2)
 
         picked_scales = sb("picked_scales", [P, S], U8)
         nc.vector.tensor_copy(out=picked_scales[:], in_=scale_table[:].indirect(offs_t[:]))
         x_plane = sb("x_plane", [P, S], U8)
         nc.vector.tensor_copy(out=x_plane[:].bitcast(I32), in_=picked_scales[:].bitcast(I32))
-        for r in range(2):
+        for r in range(1, 4):
             nc.scalar.dma_start(
-                out=x_plane[:].bitcast(I32)[2 + r : P : 32, :],
-                in_=picked_scales[:].bitcast(I32)[16 + r : P : 32, :],
+                out=x_plane[:].bitcast(I32)[r:P:32, :],
+                in_=picked_scales[:].bitcast(I32)[8 * r : P : 32, :],
             )
 
-        w2q = quantize("w2", cast_dealt(nc.vector.tensor_copy, "w2", w2_raw, "scale_table")[:], 512)
+        w2q = []
+        for u, (copy, tag) in enumerate(((nc.vector.tensor_copy, "scale_table"), (nc.scalar.copy, "w2_hi"))):
+            grouped = sb("w2_bf%d" % u, [P, 2 * 512], BF16, tag)
+            copy(
+                out=grouped[:].rearrange("p (t m j) -> p m j t", t=2, j=PACK),
+                in_=w2_raw[:].rearrange("p j (m t) -> p m j t", t=PACK)[:, :, :, 2 * u : 2 * u + 2],
+            )
+            w2q.append(quantize("w2_%d" % u, grouped[:], 256))
 
         w1_raw = load_weight("w1", w1, "w2_raw")
         w3_raw = load_weight("w3", w3, "scale_table")
@@ -118,40 +124,36 @@ def tile_picked_pnn8_relu_p_kernel(
             x_codes.append(codes)
 
         w4_raw = load_weight("w4", w4, "word_table")
-        e_banks = [psum.tile([P, S], F32, name="e_bank%d" % t, tag="a%d" % t) for t in range(PACK)]
+        e_rows = [sb("e_row%d" % t, [P, S], F32) for t in range(PACK)]
         for t, h in ((0, 0), (1, 0), (0, 1), (1, 1), (2, 0), (2, 1), (3, 0), (3, 1)):
             cols = slice(h * HALF, (h + 1) * HALF)
-            mx(e_banks[t][:, cols], w2q, slice(t * P, (t + 1) * P), x_codes[h][:], x_plane[:, cols], True, True)
-        e_rows = []
-        for t in range(PACK):
-            row = sb("e_row%d" % t, [P, S], F32)
-            nc.scalar.activation(out=row[:], in_=e_banks[t][:], func=ACT.Copy, scale=0.5)
-            e_rows.append(row)
+            bank = psum.tile([P, HALF], F32, name="e_bank%d_%d" % (t, h), tag="%s%d" % ("ab"[h], t))
+            mx(bank[:], w2q[t // 2], slice(t % 2 * P, (t % 2 + 1) * P), x_codes[h][:], x_plane[:, cols], True, True)
+            nc.scalar.activation(out=e_rows[t][:, cols], in_=bank[:], func=ACT.Copy, scale=0.5)
 
-        w1_bf = cast_dealt(nc.scalar.copy, "w1", w1_raw, "w2_codes")
+        w1_bf = cast_dealt(nc.scalar.copy, "w1", w1_raw, "w2_1_codes")
 
-        def gather_first(c, first, t):
-            j0, n = CHUNKS[c]
+        def gather_first(j0, n, first, t):
             nc.vector.tensor_copy(
                 out=first[:, t, :], in_=e_rows[t][:].indirect(p1_t[:, j0 // 16 : (j0 + n) // 16])
             )
 
-        def gather_add(c, first, both, t):
+        def gather_add(c, first, lo, both, t):
             j0, n = CHUNKS[c]
             nc.vector.tensor_tensor(
                 out=both[:, t, :],
                 in0=e_rows[t][:].indirect(p2_t[:, j0 // 16 : (j0 + n) // 16]),
-                in1=first[:, t, :],
+                in1=first[:, t, lo : lo + n],
                 op=ALU.add,
             )
 
         first0 = sb("first0", [P, PACK, 256], F32)
         both0 = sb("both0", [P, PACK, 256], F32, "both")
-        gather_first(0, first0, 0)
+        gather_first(0, 256, first0, 0)
         for t in range(1, PACK):
-            gather_first(0, first0, t)
-            gather_add(0, first0, both0, t - 1)
-        gather_add(0, first0, both0, PACK - 1)
+            gather_first(0, 256, first0, t)
+            gather_add(0, first0, 0, both0, t - 1)
+        gather_add(0, first0, 0, both0, PACK - 1)
 
         w1q = quantize("w1", w1_bf[:], 512)
         w3_bf = cast_plain(nc.scalar.copy, "w3", w3_raw)
@@ -167,15 +169,12 @@ def tile_picked_pnn8_relu_p_kernel(
                 )
             y_banks.append(bank)
 
-        y_bf = []
-        for c, (j0, n) in enumerate(CHUNKS):
-            tile = sb("y_bf%d" % c, [P, n * PACK], BF16)
-            for b in range(n // BLK):
-                nc.scalar.copy(
-                    out=tile[:, b * BLK * PACK : (b + 1) * BLK * PACK].rearrange("p (j t) -> p j t", t=PACK),
-                    in_=y_banks[j0 // BLK + b][:].rearrange("p t j -> p j t"),
-                )
-            y_bf.append(tile)
+        y_bf = sb("y_bf", [P, S * PACK], BF16)
+        for b in range(S // BLK):
+            nc.scalar.copy(
+                out=y_bf[:, b * BLK * PACK : (b + 1) * BLK * PACK].rearrange("p (j t) -> p j t", t=PACK),
+                in_=y_banks[b][:].rearrange("p t j -> p j t"),
+            )
 
         w4_bf = cast_plain(nc.scalar.copy, "w4", w4_raw)
 
@@ -197,7 +196,7 @@ def tile_picked_pnn8_relu_p_kernel(
             j0, n = CHUNKS[c]
             accs = [psum.tile([P, n], F32, name="o%d_%d" % (c, m), tag="a%d" % m) for m in range(N // P)]
             for m in range(N // P):
-                mx(accs[m][:], w3q, slice(m * P, (m + 1) * P), yq[0][:], yq[1][:], True, False)
+                mx(accs[m][:], w3q, slice(m * P, (m + 1) * P), yq[0][:, j0 : j0 + n], yq[1][:, j0 : j0 + n], True, False)
             for m in range(N // P):
                 mx(accs[m][:], w4q, slice(m * P, (m + 1) * P), zq[0][:], zq[1][:], False, True)
             last = c == len(CHUNKS) - 1
@@ -214,27 +213,31 @@ def tile_picked_pnn8_relu_p_kernel(
                     in_=res[:],
                 )
 
-        first1 = sb("first1", [P, PACK, 128], F32, "w2_codes")
+        first1 = sb("first1", [P, PACK, 256], F32, "w2_1_codes")
         for t in range(PACK):
-            gather_first(1, first1, t)
+            gather_first(256, 256, first1, t)
         z0 = product(0, both0)
         both1 = sb("both1", [P, PACK, 128], F32, "both")
         for t in range(PACK):
-            gather_add(1, first1, both1, t)
+            gather_add(1, first1, 0, both1, t)
         w3q = quantize("w3", w3_bf[:], 512)
-        yq = [quantize("y%d" % c, y_bf[c][:], CHUNKS[c][1]) for c in range(len(CHUNKS))]
+        yq = quantize("y", y_bf[:], S)
         zq0 = quantize("z0", z0[:], 256)
         z1 = product(1, both1)
-        first2 = sb("first2", [P, PACK, 128], F32, "w3_bf")
-        for t in range(PACK):
-            gather_first(2, first2, t)
         w4q = quantize("w4", w4_bf[:], 512)
         zq1 = quantize("z1", z1[:], 128)
-        finish(0, w3q, w4q, yq[0], zq0)
-        finish(1, w3q, w4q, yq[1], zq1)
+        finish(0, w3q, w4q, yq, zq0)
+        j0, n = CHUNKS[1]
+        acc1 = psum.tile([P, N // P, n], F32, name="o1", tag="b0")
+        for m in range(N // P):
+            mx(acc1[:, m, :], w3q, slice(m * P, (m + 1) * P), yq[0][:, j0 : j0 + n], yq[1][:, j0 : j0 + n], True, False)
+            mx(acc1[:, m, :], w4q, slice(m * P, (m + 1) * P), zq1[0][:], zq1[1][:], False, True)
+        res1 = sb("res1", [P, N // P, n], F32)
+        nc.scalar.activation(out=res1[:], in_=acc1[:], func=ACT.Relu)
+        nc.sync.dma_start(out=out[:, j0 : j0 + n].rearrange("(i p) j -> p i j", p=P), in_=res1[:])
         both2 = sb("both2", [P, PACK, 128], F32, "w4_bf")
         for t in range(PACK):
-            gather_add(2, first2, both2, t)
+            gather_add(2, first1, 128, both2, t)
         z2 = product(2, both2)
         zq2 = quantize("z2", z2[:], 128)
-        finish(2, w3q, w4q, yq[2], zq2)
+        finish(2, w3q, w4q, yq, zq2)

@@ -77,15 +77,11 @@ def tile_picked_pnn8_relu_p_kernel(
             )
 
         scale_table = sb("scale_table", [P, T], U8)
-        warm = sb("warm", [P, 8], F32)
-        nc.vector.memset(warm[:], 0.0)
         nc.sync.dma_start(out=offs_t[:], in_=offs)
         nc.sync.dma_start(
             out=scale_table[:].bitcast(I32),
             in_=x_scales[0].bitcast(I32).unsqueeze(1).to_broadcast([16, 8, T // 4]),
         )
-        warm2 = sb("warm2", [P, 8], F32)
-        nc.scalar.activation(out=warm2[:], in_=warm[:], func=ACT.Relu)
         w2_raw = load_weight("w2", w2)
         word_table = sb("word_table", [P, T], U32)
         nc.sync.dma_start(
@@ -104,14 +100,7 @@ def tile_picked_pnn8_relu_p_kernel(
                 in_=picked_scales[:].bitcast(I32)[8 * r : P : 32, :],
             )
 
-        w2q = []
-        for u, (copy, tag) in enumerate(((nc.vector.tensor_copy, "scale_table"), (nc.scalar.copy, "w2_hi"))):
-            grouped = sb("w2_bf%d" % u, [P, 2 * 512], BF16, tag)
-            copy(
-                out=grouped[:].rearrange("p (t m j) -> p m j t", t=2, j=PACK),
-                in_=w2_raw[:].rearrange("p j (m t) -> p m j t", t=PACK)[:, :, :, 2 * u : 2 * u + 2],
-            )
-            w2q.append(quantize("w2_%d" % u, grouped[:], 256))
+        w2q = quantize("w2", cast_dealt(nc.vector.tensor_copy, "w2", w2_raw, "scale_table")[:], 512)
 
         w1_raw = load_weight("w1", w1, "w2_raw")
         w3_raw = load_weight("w3", w3, "scale_table")
@@ -128,10 +117,10 @@ def tile_picked_pnn8_relu_p_kernel(
         for t, h in ((0, 0), (1, 0), (0, 1), (1, 1), (2, 0), (2, 1), (3, 0), (3, 1)):
             cols = slice(h * HALF, (h + 1) * HALF)
             bank = psum.tile([P, HALF], F32, name="e_bank%d_%d" % (t, h), tag="%s%d" % ("ab"[h], t))
-            mx(bank[:], w2q[t // 2], slice(t % 2 * P, (t % 2 + 1) * P), x_codes[h][:], x_plane[:, cols], True, True)
+            mx(bank[:], w2q, slice(t * P, (t + 1) * P), x_codes[h][:], x_plane[:, cols], True, True)
             nc.scalar.activation(out=e_rows[t][:, cols], in_=bank[:], func=ACT.Copy, scale=0.5)
 
-        w1_bf = cast_dealt(nc.scalar.copy, "w1", w1_raw, "w2_1_codes")
+        w1_bf = cast_dealt(nc.scalar.copy, "w1", w1_raw, "w2_codes")
 
         def gather_first(j0, n, first, t):
             nc.vector.tensor_copy(
@@ -184,10 +173,10 @@ def tile_picked_pnn8_relu_p_kernel(
             for b in range(n // BLK):
                 nc.vector.tensor_tensor(
                     out=tile[:, b * BLK * PACK : (b + 1) * BLK * PACK].rearrange(
-                        "p (c i t) -> p c t i", i=4, t=PACK
+                        "p (c i t) -> p c t i", i=2, t=PACK
                     ),
-                    in0=y_banks[j0 // BLK + b][:].rearrange("p t (c i) -> p c t i", i=4),
-                    in1=both[:, :, b * BLK : (b + 1) * BLK].rearrange("p t (c i) -> p c t i", i=4),
+                    in0=y_banks[j0 // BLK + b][:].rearrange("p t (c i) -> p c t i", i=2),
+                    in1=both[:, :, b * BLK : (b + 1) * BLK].rearrange("p t (c i) -> p c t i", i=2),
                     op=ALU.mult,
                 )
             return tile
@@ -208,12 +197,13 @@ def tile_picked_pnn8_relu_p_kernel(
                         nc.vector.tensor_scalar_max(out=res[:, i, :], in0=accs[m][:], scalar1=0.0)
                     else:
                         nc.scalar.activation(out=res[:, i, :], in_=accs[m][:], func=ACT.Relu)
-                nc.sync.dma_start(
+                queue = nc.scalar if last and pair == 0 else nc.sync
+                queue.dma_start(
                     out=out[2 * pair * P : (2 * pair + 2) * P, j0 : j0 + n].rearrange("(i p) j -> p i j", p=P),
                     in_=res[:],
                 )
 
-        first1 = sb("first1", [P, PACK, 256], F32, "w2_1_codes")
+        first1 = sb("first1", [P, PACK, 256], F32, "w2_codes")
         for t in range(PACK):
             gather_first(256, 256, first1, t)
         z0 = product(0, both0)

@@ -118,7 +118,10 @@ def tile_picked_pnn8_relu_p_kernel(
             cols = slice(h * HALF, (h + 1) * HALF)
             bank = psum.tile([P, HALF], F32, name="e_bank%d_%d" % (t, h), tag="%s%d" % ("ab"[h], t))
             mx(bank[:], w2q, slice(t * P, (t + 1) * P), x_codes[h][:], x_plane[:, cols], True, True)
-            nc.scalar.activation(out=e_rows[t][:, cols], in_=bank[:], func=ACT.Copy, scale=0.5)
+            if (t, h) == (0, 1):
+                nc.vector.tensor_scalar_mul(out=e_rows[t][:, cols], in0=bank[:], scalar1=0.5)
+            else:
+                nc.scalar.activation(out=e_rows[t][:, cols], in_=bank[:], func=ACT.Copy, scale=0.5)
 
         w1_bf = cast_dealt(nc.scalar.copy, "w1", w1_raw, "w2_codes")
 
@@ -167,9 +170,9 @@ def tile_picked_pnn8_relu_p_kernel(
 
         w4_bf = cast_plain(nc.scalar.copy, "w4", w4_raw)
 
-        def product(c, both):
+        def product(c, both, tag=None):
             j0, n = CHUNKS[c]
-            tile = sb("z_bf%d" % c, [P, n * PACK], BF16)
+            tile = sb("z_bf%d" % c, [P, n * PACK], BF16, tag)
             for b in range(n // BLK):
                 nc.vector.tensor_tensor(
                     out=tile[:, b * BLK * PACK : (b + 1) * BLK * PACK].rearrange(
@@ -203,18 +206,18 @@ def tile_picked_pnn8_relu_p_kernel(
                     in_=res[:],
                 )
 
-        first1 = sb("first1", [P, PACK, 256], F32, "w2_codes")
+        first1 = sb("first1", [P, PACK, 256], F32, "w2_raw")
         for t in range(PACK):
             gather_first(256, 256, first1, t)
-        z0 = product(0, both0)
-        both1 = sb("both1", [P, PACK, 128], F32, "both")
+        both1 = sb("both1", [P, PACK, 128], F32)
         for t in range(PACK):
             gather_add(1, first1, 0, both1, t)
         w3q = quantize("w3", w3_bf[:], 512)
+        z0 = product(0, both0)
         yq = quantize("y", y_bf[:], S)
         zq0 = quantize("z0", z0[:], 256)
-        z1 = product(1, both1)
         w4q = quantize("w4", w4_bf[:], 512)
+        z1 = product(1, both1, "word_table")
         zq1 = quantize("z1", z1[:], 128)
         finish(0, w3q, w4q, yq, zq0)
         j0, n = CHUNKS[1]

@@ -17,9 +17,15 @@ ALU = mybir.AluOpType
 
 P = 128
 PACK = 4
-BLK = 128
+WIDTH = 512
+PER_COLUMN = 16
+BLOCKS = K // 32
+BANK_PLACES = 128
 HALF = S // 2
-CHUNKS = ((0, 256), (256, 128), (384, 128))
+QUARTER = S // 4
+CHUNKS = ((0, HALF), (HALF, QUARTER), (HALF + QUARTER, QUARTER))
+LINE_F32 = 4
+LINE_PLACES = 2
 
 
 def tile_picked_pnn8_relu_p_kernel(
@@ -31,47 +37,53 @@ def tile_picked_pnn8_relu_p_kernel(
         keep = ctx.enter_context(tc.tile_pool(name="keep", bufs=1))
         psum = ctx.enter_context(tc.psum_pool(name="psum", bufs=1))
 
-        offs_t = lists.tile([P, S // 16], U16, name="offs_t")
-        p1_t = lists.tile([P, S // 16], U16, name="p1_t")
-        p2_t = lists.tile([P, S // 16], U16, name="p2_t")
+        offs_t = lists.tile([P, S // PER_COLUMN], U16, name="offs_t")
+        p1_t = lists.tile([P, S // PER_COLUMN], U16, name="p1_t")
+        p2_t = lists.tile([P, S // PER_COLUMN], U16, name="p2_t")
 
         def sb(name, shape, dtype, tag=None):
             return keep.tile(shape, dtype, name=name, tag=tag or name, align_bytes=64)
 
+        def entries(list_tile, j0, n):
+            return list_tile[:, j0 // PER_COLUMN : (j0 + n) // PER_COLUMN]
+
+        def tile_cols(i):
+            return slice(i * P, (i + 1) * P)
+
         def load_weight(name, w, tag=None):
-            raw = sb(name + "_raw", [P, PACK, 512], F32, tag)
+            raw = sb(name + "_raw", [P, PACK, WIDTH], F32, tag)
             nc.sync.dma_start(out=raw[:], in_=w.rearrange("(p j) c -> p j c", j=PACK))
             return raw
 
-        def cast_dealt(copy, name, raw, tag):
-            grouped = sb(name + "_bf", [P, PACK * 512], BF16, tag)
+        def round_dealt(copy, name, raw, tag):
+            grouped = sb(name + "_bf", [P, PACK * WIDTH], BF16, tag)
             copy(
                 out=grouped[:].rearrange("p (t m j) -> p m j t", t=PACK, j=PACK),
                 in_=raw[:].rearrange("p j (m t) -> p m j t", t=PACK),
             )
             return grouped
 
-        def cast_plain(copy, name, raw):
-            grouped = sb(name + "_bf", [P, PACK * 512], BF16)
-            copy(
-                out=grouped[:].rearrange("p (c i j) -> p c j i", i=4, j=PACK),
-                in_=raw[:].rearrange("p j (c i) -> p c j i", i=4),
+        def round_plain(name, raw):
+            grouped = sb(name + "_bf", [P, PACK * WIDTH], BF16)
+            nc.scalar.copy(
+                out=grouped[:].rearrange("p (c i j) -> p c j i", i=LINE_F32, j=PACK),
+                in_=raw[:].rearrange("p j (c i) -> p c j i", i=LINE_F32),
             )
             return grouped
 
         def quantize(name, grouped, width):
             codes = sb(name + "_codes", [P, width], U32)
             scales = sb(name + "_scales", [P, width], U8)
-            nc.vector.quantize_mx(out=codes[:].bitcast(FP8X4), scales=scales[:], in_=grouped)
+            nc.vector.quantize_mx(out=codes[:].bitcast(FP8X4), scales=scales[:], in_=grouped[:])
             return codes, scales
 
-        def mx(acc, lhs, lcols, rcodes, rscales, start, stop):
+        def mx(acc, weight, cols, moving_codes, moving_scales, start, stop):
             nc.tensor.matmul_mx(
                 out=acc,
-                lhsT=lhs[0][:, lcols].bitcast(FP8X4),
-                lhsT_scale=lhs[1][:, lcols],
-                rhs=rcodes.bitcast(FP8X4),
-                rhs_scale=rscales,
+                lhsT=weight[0][:, cols].bitcast(FP8X4),
+                lhsT_scale=weight[1][:, cols],
+                rhs=moving_codes.bitcast(FP8X4),
+                rhs_scale=moving_scales,
                 start=start,
                 stop=stop,
             )
@@ -80,7 +92,7 @@ def tile_picked_pnn8_relu_p_kernel(
         nc.sync.dma_start(out=offs_t[:], in_=offs)
         nc.sync.dma_start(
             out=scale_table[:].bitcast(I32),
-            in_=x_scales[0].bitcast(I32).unsqueeze(1).to_broadcast([16, 8, T // 4]),
+            in_=x_scales[0].bitcast(I32).unsqueeze(1).to_broadcast([BLOCKS, P // BLOCKS, T // 4]),
         )
         w2_raw = load_weight("w2", w2)
         word_table = sb("word_table", [P, T], U32)
@@ -92,145 +104,160 @@ def tile_picked_pnn8_relu_p_kernel(
 
         picked_scales = sb("picked_scales", [P, S], U8)
         nc.vector.tensor_copy(out=picked_scales[:], in_=scale_table[:].indirect(offs_t[:]))
-        x_plane = sb("x_plane", [P, S], U8)
-        nc.vector.tensor_copy(out=x_plane[:].bitcast(I32), in_=picked_scales[:].bitcast(I32))
+        x_scale_rows = sb("x_scale_rows", [P, S], U8)
+        nc.vector.tensor_copy(out=x_scale_rows[:].bitcast(I32), in_=picked_scales[:].bitcast(I32))
         for r in range(1, 4):
             nc.scalar.dma_start(
-                out=x_plane[:].bitcast(I32)[r:P:32, :],
+                out=x_scale_rows[:].bitcast(I32)[r:P:32, :],
                 in_=picked_scales[:].bitcast(I32)[8 * r : P : 32, :],
             )
 
-        w2q = quantize("w2", cast_dealt(nc.vector.tensor_copy, "w2", w2_raw, "scale_table")[:], 512)
+        w2q = quantize("w2", round_dealt(nc.vector.tensor_copy, "w2", w2_raw, "scale_table"), WIDTH)
 
         w1_raw = load_weight("w1", w1, "w2_raw")
         w3_raw = load_weight("w3", w3, "scale_table")
         x_codes = []
         for h in range(2):
             codes = sb("x_codes%d" % h, [P, HALF], U32)
-            nc.vector.tensor_copy(
-                out=codes[:], in_=word_table[:].indirect(offs_t[:, h * HALF // 16 : (h + 1) * HALF // 16])
-            )
+            nc.vector.tensor_copy(out=codes[:], in_=word_table[:].indirect(entries(offs_t, h * HALF, HALF)))
             x_codes.append(codes)
-
         w4_raw = load_weight("w4", w4, "word_table")
+
+        def picked(j0, n):
+            h, lo = divmod(j0, HALF)
+            return x_codes[h][:, lo : lo + n], x_scale_rows[:, j0 : j0 + n]
+
         e_rows = [sb("e_row%d" % t, [P, S], F32) for t in range(PACK)]
-        for t, h in ((0, 0), (1, 0), (0, 1), (1, 1), (2, 0), (2, 1), (3, 0), (3, 1)):
-            cols = slice(h * HALF, (h + 1) * HALF)
-            bank = psum.tile([P, HALF], F32, name="e_bank%d_%d" % (t, h), tag="%s%d" % ("ab"[h], t))
-            mx(bank[:], w2q, slice(t * P, (t + 1) * P), x_codes[h][:], x_plane[:, cols], True, True)
-            if (t, h) == (0, 1):
-                nc.vector.tensor_scalar_mul(out=e_rows[t][:, cols], in0=bank[:], scalar1=0.5)
+
+        def project_e(t, j0, n, bank_tag, on_vector=False):
+            bank = psum.tile([P, n], F32, name="e_bank%d_%d" % (t, j0), tag=bank_tag)
+            mx(bank[:], w2q, tile_cols(t), *picked(j0, n), True, True)
+            if on_vector:
+                nc.vector.tensor_scalar_mul(out=e_rows[t][:, j0 : j0 + n], in0=bank[:], scalar1=0.5)
             else:
-                nc.scalar.activation(out=e_rows[t][:, cols], in_=bank[:], func=ACT.Copy, scale=0.5)
+                nc.scalar.activation(out=e_rows[t][:, j0 : j0 + n], in_=bank[:], func=ACT.Copy, scale=0.5)
 
-        w1_bf = cast_dealt(nc.scalar.copy, "w1", w1_raw, "w2_codes")
+        project_e(0, 0, HALF, "a0")
+        project_e(1, 0, HALF, "a1")
+        project_e(0, HALF, QUARTER, "b0")
+        project_e(0, HALF + QUARTER, QUARTER, "b3", on_vector=True)
+        project_e(1, HALF, HALF, "b1")
+        project_e(2, 0, HALF, "a2")
+        project_e(2, HALF, HALF, "b2")
+        project_e(3, 0, HALF, "a3")
+        project_e(3, HALF, HALF, "a0")
 
-        def gather_first(j0, n, first, t):
-            nc.vector.tensor_copy(
-                out=first[:, t, :], in_=e_rows[t][:].indirect(p1_t[:, j0 // 16 : (j0 + n) // 16])
-            )
+        w1_bf = round_dealt(nc.scalar.copy, "w1", w1_raw, "w2_codes")
 
-        def gather_add(c, first, lo, both, t):
-            j0, n = CHUNKS[c]
+        def look_up_p1(dst, t, j0, n):
+            nc.vector.tensor_copy(out=dst, in_=e_rows[t][:].indirect(entries(p1_t, j0, n)))
+
+        def add_look_up_p2(mean, by_p1, t, chunk):
+            j0, n = CHUNKS[chunk]
             nc.vector.tensor_tensor(
-                out=both[:, t, :],
-                in0=e_rows[t][:].indirect(p2_t[:, j0 // 16 : (j0 + n) // 16]),
-                in1=first[:, t, lo : lo + n],
-                op=ALU.add,
+                out=mean[:, t, :], in0=e_rows[t][:].indirect(entries(p2_t, j0, n)), in1=by_p1, op=ALU.add
             )
 
-        first0 = sb("first0", [P, PACK, 256], F32)
-        both0 = sb("both0", [P, PACK, 256], F32, "both")
-        gather_first(0, 256, first0, 0)
+        by_p1_low = sb("by_p1_low", [P, PACK, HALF], F32)
+        mean0 = sb("mean0", [P, PACK, HALF], F32)
+        look_up_p1(by_p1_low[:, 0, :], 0, 0, HALF)
         for t in range(1, PACK):
-            gather_first(0, 256, first0, t)
-            gather_add(0, first0, 0, both0, t - 1)
-        gather_add(0, first0, 0, both0, PACK - 1)
+            look_up_p1(by_p1_low[:, t, :], t, 0, HALF)
+            add_look_up_p2(mean0, by_p1_low[:, t - 1, :], t - 1, 0)
+        add_look_up_p2(mean0, by_p1_low[:, PACK - 1, :], PACK - 1, 0)
 
-        w1q = quantize("w1", w1_bf[:], 512)
-        w3_bf = cast_plain(nc.scalar.copy, "w3", w3_raw)
+        w1q = quantize("w1", w1_bf, WIDTH)
+        w3_bf = round_plain("w3", w3_raw)
 
         y_banks = []
-        for b in range(S // BLK):
-            bank = psum.tile([P, PACK, BLK], F32, name="y_bank%d" % b, tag="b%d" % b)
-            h, lo = divmod(b * BLK, HALF)
+        for b in range(S // BANK_PLACES):
+            bank = psum.tile([P, PACK, BANK_PLACES], F32, name="y_bank%d" % b, tag="b%d" % b)
             for t in range(PACK):
-                mx(
-                    bank[:, t, :], w1q, slice(t * P, (t + 1) * P),
-                    x_codes[h][:, lo : lo + BLK], x_plane[:, b * BLK : (b + 1) * BLK], True, True,
-                )
+                mx(bank[:, t, :], w1q, tile_cols(t), *picked(b * BANK_PLACES, BANK_PLACES), True, True)
             y_banks.append(bank)
 
         y_bf = sb("y_bf", [P, S * PACK], BF16)
-        for b in range(S // BLK):
+        for b in range(S // BANK_PLACES):
             nc.scalar.copy(
-                out=y_bf[:, b * BLK * PACK : (b + 1) * BLK * PACK].rearrange("p (j t) -> p j t", t=PACK),
+                out=y_bf[:, b * BANK_PLACES * PACK : (b + 1) * BANK_PLACES * PACK].rearrange(
+                    "p (j t) -> p j t", t=PACK
+                ),
                 in_=y_banks[b][:].rearrange("p t j -> p j t"),
             )
 
-        w4_bf = cast_plain(nc.scalar.copy, "w4", w4_raw)
+        w4_bf = round_plain("w4", w4_raw)
 
-        def product(c, both, tag=None):
-            j0, n = CHUNKS[c]
-            tile = sb("z_bf%d" % c, [P, n * PACK], BF16, tag)
-            for b in range(n // BLK):
-                nc.vector.tensor_tensor(
-                    out=tile[:, b * BLK * PACK : (b + 1) * BLK * PACK].rearrange(
-                        "p (c i t) -> p c t i", i=2, t=PACK
-                    ),
-                    in0=y_banks[j0 // BLK + b][:].rearrange("p t (c i) -> p c t i", i=2),
-                    in1=both[:, :, b * BLK : (b + 1) * BLK].rearrange("p t (c i) -> p c t i", i=2),
-                    op=ALU.mult,
-                )
-            return tile
+        def multiply(z_bf, mean, chunk, lo, n):
+            b, in_bank = divmod(CHUNKS[chunk][0] + lo, BANK_PLACES)
+            nc.vector.tensor_tensor(
+                out=z_bf[:, lo * PACK : (lo + n) * PACK].rearrange("p (c i t) -> p c t i", i=LINE_PLACES, t=PACK),
+                in0=y_banks[b][:, :, in_bank : in_bank + n].rearrange("p t (c i) -> p c t i", i=LINE_PLACES),
+                in1=mean[:, :, lo : lo + n].rearrange("p t (c i) -> p c t i", i=LINE_PLACES),
+                op=ALU.mult,
+            )
 
-        def finish(c, w3q, w4q, yq, zq):
-            j0, n = CHUNKS[c]
-            accs = [psum.tile([P, n], F32, name="o%d_%d" % (c, m), tag="a%d" % m) for m in range(N // P)]
+        def finish_by_banks(chunk, zq, share_with_vector):
+            j0, n = CHUNKS[chunk]
+            accs = [psum.tile([P, n], F32, name="o%d_%d" % (chunk, m), tag="a%d" % m) for m in range(N // P)]
             for m in range(N // P):
-                mx(accs[m][:], w3q, slice(m * P, (m + 1) * P), yq[0][:, j0 : j0 + n], yq[1][:, j0 : j0 + n], True, False)
+                mx(accs[m][:], w3q, tile_cols(m), yq[0][:, j0 : j0 + n], yq[1][:, j0 : j0 + n], True, False)
             for m in range(N // P):
-                mx(accs[m][:], w4q, slice(m * P, (m + 1) * P), zq[0][:], zq[1][:], False, True)
-            last = c == len(CHUNKS) - 1
+                mx(accs[m][:], w4q, tile_cols(m), zq[0][:], zq[1][:], False, True)
             for pair in range(2):
-                res = sb("res%d_%d" % (c, pair), [P, 2, n], F32)
+                res = sb("res%d_%d" % (chunk, pair), [P, 2, n], F32)
                 for i in range(2):
-                    m = 2 * pair + i
-                    if last and pair == 1:
-                        nc.vector.tensor_scalar_max(out=res[:, i, :], in0=accs[m][:], scalar1=0.0)
+                    acc = accs[2 * pair + i]
+                    if share_with_vector and pair == 1:
+                        nc.vector.tensor_scalar_max(out=res[:, i, :], in0=acc[:], scalar1=0.0)
                     else:
-                        nc.scalar.activation(out=res[:, i, :], in_=accs[m][:], func=ACT.Relu)
-                queue = nc.scalar if last and pair == 0 else nc.sync
+                        nc.scalar.activation(out=res[:, i, :], in_=acc[:], func=ACT.Relu)
+                queue = nc.scalar if share_with_vector and pair == 0 else nc.sync
                 queue.dma_start(
                     out=out[2 * pair * P : (2 * pair + 2) * P, j0 : j0 + n].rearrange("(i p) j -> p i j", p=P),
                     in_=res[:],
                 )
 
-        first1 = sb("first1", [P, PACK, 256], F32, "w2_raw")
+        def finish_in_one_bank(chunk, zq):
+            j0, n = CHUNKS[chunk]
+            acc = psum.tile([P, N // P, n], F32, name="o%d" % chunk, tag="b0")
+            for m in range(N // P):
+                mx(acc[:, m, :], w3q, tile_cols(m), yq[0][:, j0 : j0 + n], yq[1][:, j0 : j0 + n], True, False)
+                mx(acc[:, m, :], w4q, tile_cols(m), zq[0][:], zq[1][:], False, True)
+            res = sb("res%d" % chunk, [P, N // P, n], F32)
+            nc.scalar.activation(out=res[:], in_=acc[:], func=ACT.Relu)
+            nc.sync.dma_start(out=out[:, j0 : j0 + n].rearrange("(i p) j -> p i j", p=P), in_=res[:])
+
+        by_p1_high = sb("by_p1_high", [P, PACK, HALF], F32, "w2_raw")
         for t in range(PACK):
-            gather_first(256, 256, first1, t)
-        both1 = sb("both1", [P, PACK, 128], F32)
+            look_up_p1(by_p1_high[:, t, :], t, HALF, HALF)
+        mean1 = sb("mean1", [P, PACK, QUARTER], F32)
         for t in range(PACK):
-            gather_add(1, first1, 0, both1, t)
-        w3q = quantize("w3", w3_bf[:], 512)
-        z0 = product(0, both0)
-        yq = quantize("y", y_bf[:], S)
-        zq0 = quantize("z0", z0[:], 256)
-        w4q = quantize("w4", w4_bf[:], 512)
-        z1 = product(1, both1, "word_table")
-        zq1 = quantize("z1", z1[:], 128)
-        finish(0, w3q, w4q, yq, zq0)
-        j0, n = CHUNKS[1]
-        acc1 = psum.tile([P, N // P, n], F32, name="o1", tag="b0")
-        for m in range(N // P):
-            mx(acc1[:, m, :], w3q, slice(m * P, (m + 1) * P), yq[0][:, j0 : j0 + n], yq[1][:, j0 : j0 + n], True, False)
-            mx(acc1[:, m, :], w4q, slice(m * P, (m + 1) * P), zq1[0][:], zq1[1][:], False, True)
-        res1 = sb("res1", [P, N // P, n], F32)
-        nc.scalar.activation(out=res1[:], in_=acc1[:], func=ACT.Relu)
-        nc.sync.dma_start(out=out[:, j0 : j0 + n].rearrange("(i p) j -> p i j", p=P), in_=res1[:])
-        both2 = sb("both2", [P, PACK, 128], F32, "w4_bf")
+            add_look_up_p2(mean1, by_p1_high[:, t, :QUARTER], t, 1)
+        w3q = quantize("w3", w3_bf, WIDTH)
+        z0_bf = sb("z0_bf", [P, HALF * PACK], BF16)
+        for lo in range(0, HALF, BANK_PLACES):
+            multiply(z0_bf, mean0, 0, lo, BANK_PLACES)
+        yq = quantize("y", y_bf, S)
+        z0q = quantize("z0", z0_bf, HALF)
+        w4q = quantize("w4", w4_bf, WIDTH)
+        z1_bf = sb("z1_bf", [P, QUARTER * PACK], BF16, "word_table")
+        multiply(z1_bf, mean1, 1, 0, QUARTER)
+        z1q = quantize("z1", z1_bf, QUARTER)
+        finish_by_banks(0, z0q, share_with_vector=False)
+        finish_in_one_bank(1, z1q)
+
+        mean2 = sb("mean2", [P, PACK, QUARTER], F32, "w4_bf")
         for t in range(PACK):
-            gather_add(2, first1, 128, both2, t)
-        z2 = product(2, both2)
-        zq2 = quantize("z2", z2[:], 128)
-        finish(2, w3q, w4q, yq, zq2)
+            add_look_up_p2(mean2, by_p1_high[:, t, QUARTER:], t, 2)
+        part = QUARTER // 2
+        z2_bf = sb("z2_bf", [P, QUARTER * PACK], BF16)
+        z2q = (sb("z2_codes", [P, QUARTER], U32), sb("z2_scales", [P, QUARTER], U8))
+        for lo in (0, part):
+            multiply(z2_bf, mean2, 2, lo, part)
+        for lo in (0, part):
+            nc.vector.quantize_mx(
+                out=z2q[0][:, lo : lo + part].bitcast(FP8X4),
+                scales=z2q[1][:, lo : lo + part],
+                in_=z2_bf[:, lo * PACK : (lo + part) * PACK],
+            )
+        finish_by_banks(2, z2q, share_with_vector=True)

from contextlib import ExitStack

import concourse.mybir as mybir

K, T, S, N, H = 512, 2048, 512, 512, 512
FLOPS = 2 * K * H * S * 2 + 2 * H * N * S * 2

F32 = mybir.dt.float32
BF16 = mybir.dt.bfloat16
I32 = mybir.dt.int32
U32 = mybir.dt.uint32
U16 = mybir.dt.uint16
U8 = mybir.dt.uint8
FP8X4 = mybir.dt.float8_e4m3fn_x4
ACT = mybir.ActivationFunctionType
ALU = mybir.AluOpType

P = 128
PACK = 4
WIDTH = 512
PER_COLUMN = 16
BLOCKS = K // 32
BANK_PLACES = 128
HALF = S // 2
QUARTER = S // 4
CHUNKS = ((0, HALF), (HALF, QUARTER), (HALF + QUARTER, QUARTER))
LINE_F32 = 4
LINE_PLACES = 2


def tile_picked_pnn8_relu_p_kernel(
    tc, x_words, x_scales, w1, w2, w3, w4, offs, p1, p2, out
):
    nc = tc.nc
    with ExitStack() as ctx:
        lists = ctx.enter_context(tc.tile_pool(name="lists", bufs=1))
        keep = ctx.enter_context(tc.tile_pool(name="keep", bufs=1))
        psum = ctx.enter_context(tc.psum_pool(name="psum", bufs=1))

        offs_t = lists.tile([P, S // PER_COLUMN], U16, name="offs_t")
        p1_t = lists.tile([P, S // PER_COLUMN], U16, name="p1_t")
        p2_t = lists.tile([P, S // PER_COLUMN], U16, name="p2_t")

        def sb(name, shape, dtype, tag=None):
            return keep.tile(shape, dtype, name=name, tag=tag or name, align_bytes=64)

        def entries(list_tile, j0, n):
            return list_tile[:, j0 // PER_COLUMN : (j0 + n) // PER_COLUMN]

        def tile_cols(i):
            return slice(i * P, (i + 1) * P)

        def load_weight(name, w, tag=None):
            raw = sb(name + "_raw", [P, PACK, WIDTH], F32, tag)
            nc.sync.dma_start(out=raw[:], in_=w.rearrange("(p j) c -> p j c", j=PACK))
            return raw

        def round_dealt(copy, name, raw, tag):
            grouped = sb(name + "_bf", [P, PACK * WIDTH], BF16, tag)
            copy(
                out=grouped[:].rearrange("p (t m j) -> p m j t", t=PACK, j=PACK),
                in_=raw[:].rearrange("p j (m t) -> p m j t", t=PACK),
            )
            return grouped

        def round_plain(name, raw):
            grouped = sb(name + "_bf", [P, PACK * WIDTH], BF16)
            nc.scalar.copy(
                out=grouped[:].rearrange("p (c i j) -> p c j i", i=LINE_F32, j=PACK),
                in_=raw[:].rearrange("p j (c i) -> p c j i", i=LINE_F32),
            )
            return grouped

        def quantize(name, grouped, width):
            codes = sb(name + "_codes", [P, width], U32)
            scales = sb(name + "_scales", [P, width], U8)
            nc.vector.quantize_mx(out=codes[:].bitcast(FP8X4), scales=scales[:], in_=grouped[:])
            return codes, scales

        def mx(acc, weight, cols, moving_codes, moving_scales, start, stop):
            nc.tensor.matmul_mx(
                out=acc,
                lhsT=weight[0][:, cols].bitcast(FP8X4),
                lhsT_scale=weight[1][:, cols],
                rhs=moving_codes.bitcast(FP8X4),
                rhs_scale=moving_scales,
                start=start,
                stop=stop,
            )

        scale_table = sb("scale_table", [P, T], U8)
        nc.sync.dma_start(out=offs_t[:], in_=offs)
        nc.sync.dma_start(
            out=scale_table[:].bitcast(I32),
            in_=x_scales[0].bitcast(I32).unsqueeze(1).to_broadcast([BLOCKS, P // BLOCKS, T // 4]),
        )
        w2_raw = load_weight("w2", w2)
        word_table = sb("word_table", [P, T], U32)
        nc.sync.dma_start(
            out=word_table[:].bitcast(I32), in_=x_words[0].rearrange("p n t -> p (n t)").bitcast(I32)
        )
        nc.sync.dma_start(out=p1_t[:], in_=p1)
        nc.sync.dma_start(out=p2_t[:], in_=p2)

        picked_scales = sb("picked_scales", [P, S], U8)
        nc.vector.tensor_copy(out=picked_scales[:], in_=scale_table[:].indirect(offs_t[:]))
        x_scale_rows = sb("x_scale_rows", [P, S], U8)
        nc.vector.tensor_copy(out=x_scale_rows[:].bitcast(I32), in_=picked_scales[:].bitcast(I32))
        for r in range(1, 4):
            nc.scalar.dma_start(
                out=x_scale_rows[:].bitcast(I32)[r:P:32, :],
                in_=picked_scales[:].bitcast(I32)[8 * r : P : 32, :],
            )

        w2q = quantize("w2", round_dealt(nc.vector.tensor_copy, "w2", w2_raw, "scale_table"), WIDTH)

        w1_raw = load_weight("w1", w1, "w2_raw")
        w3_raw = load_weight("w3", w3, "scale_table")
        x_codes = []
        for h in range(2):
            codes = sb("x_codes%d" % h, [P, HALF], U32)
            nc.vector.tensor_copy(out=codes[:], in_=word_table[:].indirect(entries(offs_t, h * HALF, HALF)))
            x_codes.append(codes)
        w4_raw = load_weight("w4", w4, "word_table")

        def picked(j0, n):
            h, lo = divmod(j0, HALF)
            return x_codes[h][:, lo : lo + n], x_scale_rows[:, j0 : j0 + n]

        e_rows = [sb("e_row%d" % t, [P, S], F32) for t in range(PACK)]

        def project_e(t, j0, n, bank_tag, on_vector=False):
            bank = psum.tile([P, n], F32, name="e_bank%d_%d" % (t, j0), tag=bank_tag)
            mx(bank[:], w2q, tile_cols(t), *picked(j0, n), True, True)
            if on_vector:
                nc.vector.tensor_scalar_mul(out=e_rows[t][:, j0 : j0 + n], in0=bank[:], scalar1=0.5)
            else:
                nc.scalar.activation(out=e_rows[t][:, j0 : j0 + n], in_=bank[:], func=ACT.Copy, scale=0.5)

        project_e(0, 0, HALF, "a0")
        project_e(1, 0, HALF, "a1")
        project_e(0, HALF, QUARTER, "b0")
        project_e(0, HALF + QUARTER, QUARTER, "b3", on_vector=True)
        project_e(1, HALF, HALF, "b1")
        project_e(2, 0, HALF, "a2")
        project_e(2, HALF, HALF, "b2")
        project_e(3, 0, HALF, "a3")
        project_e(3, HALF, HALF, "a0")

        w1_bf = round_dealt(nc.scalar.copy, "w1", w1_raw, "w2_codes")

        def look_up_p1(dst, t, j0, n):
            nc.vector.tensor_copy(out=dst, in_=e_rows[t][:].indirect(entries(p1_t, j0, n)))

        def add_look_up_p2(mean, by_p1, t, chunk):
            j0, n = CHUNKS[chunk]
            nc.vector.tensor_tensor(
                out=mean[:, t, :], in0=e_rows[t][:].indirect(entries(p2_t, j0, n)), in1=by_p1, op=ALU.add
            )

        by_p1_low = sb("by_p1_low", [P, PACK, HALF], F32)
        mean0 = sb("mean0", [P, PACK, HALF], F32)
        look_up_p1(by_p1_low[:, 0, :], 0, 0, HALF)
        for t in range(1, PACK):
            look_up_p1(by_p1_low[:, t, :], t, 0, HALF)
            add_look_up_p2(mean0, by_p1_low[:, t - 1, :], t - 1, 0)
        add_look_up_p2(mean0, by_p1_low[:, PACK - 1, :], PACK - 1, 0)

        w1q = quantize("w1", w1_bf, WIDTH)
        w3_bf = round_plain("w3", w3_raw)

        y_banks = []
        for b in range(S // BANK_PLACES):
            bank = psum.tile([P, PACK, BANK_PLACES], F32, name="y_bank%d" % b, tag="b%d" % b)
            for t in range(PACK):
                mx(bank[:, t, :], w1q, tile_cols(t), *picked(b * BANK_PLACES, BANK_PLACES), True, True)
            y_banks.append(bank)

        y_bf = sb("y_bf", [P, S * PACK], BF16)
        for b in range(S // BANK_PLACES):
            nc.scalar.copy(
                out=y_bf[:, b * BANK_PLACES * PACK : (b + 1) * BANK_PLACES * PACK].rearrange(
                    "p (j t) -> p j t", t=PACK
                ),
                in_=y_banks[b][:].rearrange("p t j -> p j t"),
            )

        w4_bf = round_plain("w4", w4_raw)

        def multiply(z_bf, mean, chunk, lo, n):
            b, in_bank = divmod(CHUNKS[chunk][0] + lo, BANK_PLACES)
            nc.vector.tensor_tensor(
                out=z_bf[:, lo * PACK : (lo + n) * PACK].rearrange("p (c i t) -> p c t i", i=LINE_PLACES, t=PACK),
                in0=y_banks[b][:, :, in_bank : in_bank + n].rearrange("p t (c i) -> p c t i", i=LINE_PLACES),
                in1=mean[:, :, lo : lo + n].rearrange("p t (c i) -> p c t i", i=LINE_PLACES),
                op=ALU.mult,
            )

        def finish_by_banks(chunk, zq, share_with_vector):
            j0, n = CHUNKS[chunk]
            accs = [psum.tile([P, n], F32, name="o%d_%d" % (chunk, m), tag="a%d" % m) for m in range(N // P)]
            for m in range(N // P):
                mx(accs[m][:], w3q, tile_cols(m), yq[0][:, j0 : j0 + n], yq[1][:, j0 : j0 + n], True, False)
            for m in range(N // P):
                mx(accs[m][:], w4q, tile_cols(m), zq[0][:], zq[1][:], False, True)
            for pair in range(2):
                res = sb("res%d_%d" % (chunk, pair), [P, 2, n], F32)
                for i in range(2):
                    acc = accs[2 * pair + i]
                    if share_with_vector and pair == 1:
                        nc.vector.tensor_scalar_max(out=res[:, i, :], in0=acc[:], scalar1=0.0)
                    else:
                        nc.scalar.activation(out=res[:, i, :], in_=acc[:], func=ACT.Relu)
                queue = nc.scalar if share_with_vector and pair == 0 else nc.sync
                queue.dma_start(
                    out=out[2 * pair * P : (2 * pair + 2) * P, j0 : j0 + n].rearrange("(i p) j -> p i j", p=P),
                    in_=res[:],
                )

        def finish_in_one_bank(chunk, zq):
            j0, n = CHUNKS[chunk]
            acc = psum.tile([P, N // P, n], F32, name="o%d" % chunk, tag="b0")
            for m in range(N // P):
                mx(acc[:, m, :], w3q, tile_cols(m), yq[0][:, j0 : j0 + n], yq[1][:, j0 : j0 + n], True, False)
                mx(acc[:, m, :], w4q, tile_cols(m), zq[0][:], zq[1][:], False, True)
            res = sb("res%d" % chunk, [P, N // P, n], F32)
            nc.scalar.activation(out=res[:], in_=acc[:], func=ACT.Relu)
            nc.sync.dma_start(out=out[:, j0 : j0 + n].rearrange("(i p) j -> p i j", p=P), in_=res[:])

        by_p1_high = sb("by_p1_high", [P, PACK, HALF], F32, "w2_raw")
        for t in range(PACK):
            look_up_p1(by_p1_high[:, t, :], t, HALF, HALF)
        mean1 = sb("mean1", [P, PACK, QUARTER], F32)
        for t in range(PACK):
            add_look_up_p2(mean1, by_p1_high[:, t, :QUARTER], t, 1)
        w3q = quantize("w3", w3_bf, WIDTH)
        z0_bf = sb("z0_bf", [P, HALF * PACK], BF16)
        for lo in range(0, HALF, BANK_PLACES):
            multiply(z0_bf, mean0, 0, lo, BANK_PLACES)
        yq = quantize("y", y_bf, S)
        z0q = quantize("z0", z0_bf, HALF)
        w4q = quantize("w4", w4_bf, WIDTH)
        z1_bf = sb("z1_bf", [P, QUARTER * PACK], BF16, "word_table")
        multiply(z1_bf, mean1, 1, 0, QUARTER)
        z1q = quantize("z1", z1_bf, QUARTER)
        finish_by_banks(0, z0q, share_with_vector=False)
        finish_in_one_bank(1, z1q)

        mean2 = sb("mean2", [P, PACK, QUARTER], F32, "w4_bf")
        for t in range(PACK):
            add_look_up_p2(mean2, by_p1_high[:, t, QUARTER:], t, 2)
        part = QUARTER // 2
        z2_bf = sb("z2_bf", [P, QUARTER * PACK], BF16)
        z2q = (sb("z2_codes", [P, QUARTER], U32), sb("z2_scales", [P, QUARTER], U8))
        for lo in (0, part):
            multiply(z2_bf, mean2, 2, lo, part)
        for lo in (0, part):
            nc.vector.quantize_mx(
                out=z2q[0][:, lo : lo + part].bitcast(FP8X4),
                scales=z2q[1][:, lo : lo + part],
                in_=z2_bf[:, lo * PACK : (lo + part) * PACK],
            )
        finish_by_banks(2, z2q, share_with_vector=True)
